import numpy as np
import ml_dtypes


def mxq(x, axis, fmt="e4m3"):
    dtype, down = {"e4m3": (ml_dtypes.float8_e4m3fn, 7), "e5m2": (ml_dtypes.float8_e5m2, 14)}[fmt]
    v = np.moveaxis(np.asarray(x, np.float32).astype(ml_dtypes.bfloat16).astype(np.float64), axis, -1)
    blocks = v.reshape(v.shape[:-1] + (-1, 32))
    amax = np.abs(blocks).max(-1, keepdims=True)
    byte = np.maximum(np.where(amax > 0, np.frexp(amax)[1] - 1 + 127, 0) - down, 1)
    scale = np.exp2(byte - 127.0)
    codes = (blocks / scale).astype(np.float32).astype(dtype).astype(np.float64)
    return np.moveaxis((codes * scale).reshape(v.shape), -1, axis)


WIDE = False


def mx_kscale(k):
    if not WIDE:
        return np.ones(k)
    levels = np.array([10, -10, 5, -5, 0])
    if k % 512:
        return np.exp2(np.random.permutation(np.resize(levels, k // 32))).repeat(32)
    a = np.empty((k // 512, 16))
    for p in range(k // 512):
        a[p, :8] = np.random.permutation(np.resize(levels, 8))
        for g in range(8):
            far = levels[np.abs(levels - a[p, g]) >= 10]
            a[p, g + 8] = far[np.random.randint(len(far))]
    return np.exp2(a.ravel()).repeat(32)


def f64(x):
    return np.asarray(x).astype(np.float64)


def striped(idx):
    return np.tile(idx.reshape(-1, 16).T, (8, 1)).astype(np.uint16)


def unstriped(offs):
    return offs[:16].T.reshape(-1).astype(np.int64)


def striped8(idx):
    return np.concatenate([x.reshape(-1, 16).T for x in idx]).astype(np.uint16)


def runs(offs, k):
    lists = np.stack([offs[16 * r : 16 * r + 16].T.reshape(-1) for r in range(8)]).astype(np.int64)
    return lists[np.arange(k) % 512 // 64]


def pack_weight(w):
    k, n = w.shape
    w = f64(np.asarray(w, np.float32).astype(ml_dtypes.bfloat16)).reshape(k // 32, 32, n)
    amax = np.abs(w).max(1)
    byte = np.clip(np.where(amax > 0, np.frexp(amax)[1] - 1 + 127 - 7, 1), 1, 254)
    scaled = (w * np.exp2(127.0 - byte)[:, None, :]).reshape(k, n).astype(np.float32)
    words = np.ascontiguousarray(scaled.reshape(k // 512, 128, 4, n).transpose(0, 1, 3, 2)).astype(ml_dtypes.float8_e4m3fn).view(np.uint8)
    return words, np.ascontiguousarray(byte.astype(np.uint8).reshape(k // 512, 16, n))


def unpack_weight(words, scales):
    g, p, n, _ = words.shape
    vals = np.ascontiguousarray(words).view(ml_dtypes.float8_e4m3fn).astype(np.float64) * np.repeat(np.exp2(scales.astype(np.float64) - 127.0), 8, axis=1)[..., None]
    return vals.transpose(0, 1, 3, 2).reshape(g * 512, n)


def sigmoid(v):
    return 1.0 / (1.0 + np.exp(-np.maximum(v, -700.0)))


K, T, S, H = 512, 2048, 512, 512


def setup_inputs():
    n = np.random.standard_normal
    s = mx_kscale(K)[:, None]
    u = mx_kscale(H)
    packed_xT = pack_weight(n((K, T)) * s)
    return {
        "x_words": packed_xT[0],
        "x_scales": packed_xT[1],
        "w1": (n((K, H)) / np.sqrt(K) / s).astype(np.float32),
        "gn": (np.random.uniform(0.5, 1.5, (H, 1)) * u[:, None]).astype(np.float32),
        "w2": (n((H, H)) / np.sqrt(H) / u[:, None]).astype(np.float32),
        "offs": striped(np.random.permutation(T)[:S]),
        "n1": striped8(np.stack([np.random.permutation(S) for _ in range(8)])),
        "n2": striped8(np.stack([np.random.permutation(S) for _ in range(8)])),
        "n3": striped8(np.stack([np.random.permutation(S) for _ in range(8)])),
        "n4": striped8(np.stack([np.random.permutation(S) for _ in range(8)])),
        "n5": striped8(np.stack([np.random.permutation(S) for _ in range(8)])),
        "n6": striped8(np.stack([np.random.permutation(S) for _ in range(8)])),
    }


def reference(x_words, x_scales, w1, gn, w2, offs, n1, n2, n3, n4, n5, n6):
    xq = unpack_weight(x_words, x_scales)[:, unstriped(offs)]
    y = mxq(f64(w1), 0, "e4m3").T @ xq
    z = f64(gn) * (0.75 * (y[np.arange(H)[:, None], runs(n1, H)] + y[np.arange(H)[:, None], runs(n2, H)]) - y)
    w2q = mxq(f64(w2), 0, "e4m3")
    a = w2q.T @ mxq(z, 0, "e4m3")
    z2 = f64(gn) * (y - (np.minimum(y[np.arange(H)[:, None], runs(n3, H)], y[np.arange(H)[:, None], runs(n4, H)])))
    b = w2q.T @ mxq(z2, 0, "e4m3")
    return a + (sigmoid(b[np.arange(H)[:, None], runs(n6, H)] - b)) * (a[np.arange(H)[:, None], runs(n5, H)] - a)

@@ -1,0 +1,227 @@
+from contextlib import ExitStack
+
+import concourse.mybir as mybir
+
+K, T, S, H = 512, 2048, 512, 512
+FLOPS = 3 * 2 * 512 * 512 * 512
+
+F32 = mybir.dt.float32
+BF16 = mybir.dt.bfloat16
+I32 = mybir.dt.int32
+U32 = mybir.dt.uint32
+U16 = mybir.dt.uint16
+U8 = mybir.dt.uint8
+X4 = mybir.dt.float8_e4m3fn_x4
+ALU = mybir.AluOpType
+ACT = mybir.ActivationFunctionType
+
+P = 128
+PACK = 4
+HALF = S // 2
+HCOL = HALF // 16
+
+
+def tile_picked_tiepullblapunder_none_p_kernel(tc, x_words, x_scales, w1, gn, w2, offs, n1, n2, n3, n4, n5, n6, out):
+    nc = tc.nc
+    with ExitStack() as ctx:
+        lists = ctx.enter_context(tc.tile_pool(name="lists", bufs=1))
+        sb = ctx.enter_context(tc.tile_pool(name="sb", bufs=1))
+        ps = ctx.enter_context(tc.psum_pool(name="ps", bufs=1))
+
+        def load_list(name, src):
+            tl = lists.tile([P, S // 16], U16, name=name)
+            nc.sync.dma_start(tl[:], src)
+            return tl
+
+        def half(h):
+            return slice(h * HALF, (h + 1) * HALF)
+
+        def pick(window, lst, h):
+            return window[:].indirect(lst[:, h * HCOL:(h + 1) * HCOL])
+
+        xs = sb.tile([P, T], U8, name="xs", align_bytes=64)
+        nc.vector.memset(xs[:].bitcast(I32), 0)
+        g = sb.tile([P, PACK], F32, name="g")
+        for q in range(4):
+            nc.scalar.dma_start(xs[32 * q:32 * q + 4, :].bitcast(I32), x_scales[0, 4 * q:4 * q + 4, :].bitcast(I32))
+        w1r = sb.tile([P, PACK, H], F32, name="w1r", tag="wraw")
+        nc.sync.dma_start(w1r[:], w1.rearrange("(p j) c -> p j c", j=PACK))
+        lo = load_list("lo", offs)
+        xw = sb.tile([P, T], U32, name="xw", align_bytes=64)
+        nc.sync.dma_start(xw[:].bitcast(I32), x_words[0].rearrange("p n r -> p (n r)").bitcast(I32))
+        nc.sync.dma_start(g[:], gn.rearrange("(p t) o -> p (t o)", t=PACK))
+        l3 = load_list("l3", n3)
+        l4 = load_list("l4", n4)
+        l1 = load_list("l1", n1)
+        l2 = load_list("l2", n2)
+        l6 = load_list("l6", n6)
+        l5 = load_list("l5", n5)
+
+        sg = sb.tile([P, PACK], F32, name="sg")
+        sg2 = sb.tile([P, PACK], F32, name="sg2")
+        ga = sb.tile([P, PACK], F32, name="ga")
+        ga75 = sb.tile([P, PACK], F32, name="ga75")
+        warm = sb.tile([P, PACK], F32, name="warm")
+        nc.scalar.activation(warm[:], g[:], ACT.Sigmoid)
+        nc.vector.tensor_scalar(sg2[:], g[:], 0.0, 2.0, ALU.is_ge, ALU.mult)
+        nc.vector.tensor_scalar(sg[:], sg2[:], -1.0, None, ALU.add)
+        nc.vector.tensor_tensor(ga[:], g[:], sg[:], ALU.mult)
+        nc.vector.tensor_scalar(ga75[:], ga[:], 0.75, None, ALU.mult)
+
+        xsg = sb.tile([P, S], U8, name="xsg", align_bytes=64)
+        nc.vector.tensor_copy(xsg[:], xs[:].indirect(lo[:]))
+        w1g = sb.tile([P, PACK * H], BF16, name="w1g", align_bytes=64)
+        nc.vector.tensor_copy(w1g[:].rearrange("p (t m j) -> p m j t", t=PACK, j=PACK),
+                              w1r[:].rearrange("p j (m t) -> p m j t", t=PACK))
+        w2r = sb.tile([P, PACK, H], F32, name="w2r", tag="wraw")
+        nc.sync.dma_start(w2r[:], w2.rearrange("(p j) c -> p j c", j=PACK))
+        w1c = sb.tile([P, H], U32, name="w1c", align_bytes=64)
+        w1s = sb.tile([P, H], U8, name="w1s", align_bytes=64)
+        nc.vector.quantize_mx(w1c[:].bitcast(X4), w1s[:], w1g[:])
+        xwg = sb.tile([P, S], U32, name="xwg", align_bytes=64)
+        nc.vector.tensor_copy(xwg[:], xw[:].indirect(lo[:]))
+
+        yb = []
+        for t in range(PACK):
+            bank = ps.tile([P, S], F32, name=f"y{t}", tag=f"bankA{t}")
+            cols = slice(t * P, (t + 1) * P)
+            nc.tensor.matmul_mx(bank[:], lhsT=w1c[:, cols].bitcast(X4), lhsT_scale=w1s[:, cols],
+                                rhs=xwg[:].bitcast(X4), rhs_scale=xsg[:], start=True, stop=True)
+            yb.append(bank)
+        hw, hp, ww = [], [], []
+        for t in range(PACK):
+            a_ = sb.tile([P, S], F32, name=f"hw{t}")
+            b_ = sb.tile([P, S], F32, name=f"hp{t}")
+            nc.scalar.activation(a_[:], yb[t][:], ACT.Copy, scale=ga[:, t:t + 1])
+            nc.scalar.activation(b_[:], yb[t][:], ACT.Copy, scale=ga[:, t:t + 1])
+            hw.append(a_)
+            hp.append(b_)
+        for t in range(PACK):
+            c_ = sb.tile([P, S], F32, name=f"ww{t}")
+            nc.scalar.activation(c_[:], yb[t][:], ACT.Copy, scale=ga75[:, t:t + 1])
+            ww.append(c_)
+
+        w2p = sb.tile([P, PACK, H], BF16, name="w2p")
+        for j in range(PACK):
+            nc.scalar.activation(w2p[:, j, :], w2r[:, j, :], ACT.Copy, scale=sg[:, j:j + 1])
+        w2g = sb.tile([P, PACK * H], BF16, name="w2g", tag="tB", align_bytes=64)
+        nc.scalar.copy(w2g[:].rearrange("p (t m j) -> p m j t", t=PACK, j=PACK),
+                       w2p[:].rearrange("p j (m t) -> p m j t", t=PACK))
+        w2c = sb.tile([P, H], U32, name="w2c", align_bytes=64)
+        w2s = sb.tile([P, H], U8, name="w2s", align_bytes=64)
+
+        def interleave(grp, planes):
+            nc.scalar.copy(grp.rearrange("p (c i t) -> p c t i", i=4, t=PACK),
+                           planes[:].rearrange("p t (c i) -> p c t i", i=4))
+
+        def quantize(name, grp, width, tag):
+            codes = sb.tile([P, width], U32, name=name + "c", tag=tag, align_bytes=64)
+            scales = sb.tile([P, width], U8, name=name + "s", align_bytes=64)
+            nc.vector.quantize_mx(codes[:].bitcast(X4), scales[:], grp[:])
+            return codes, scales
+
+        def second(banks, cs, codes, scales):
+            for t in range(PACK):
+                cols = slice(t * P, (t + 1) * P)
+                nc.tensor.matmul_mx(banks[t][:, cs], lhsT=w2c[:, cols].bitcast(X4), lhsT_scale=w2s[:, cols],
+                                    rhs=codes[:].bitcast(X4), rhs_scale=scales[:], start=True, stop=True)
+
+        def planes(name, tag, dt=F32):
+            return sb.tile([P, PACK, HALF], dt, name=name, tag=tag, align_bytes=64)
+
+        d3 = [planes("d3_0", "d3_0"), planes("d3_1", "tA")]
+        d4 = [planes("d4_0", "d4_0"), planes("d4_1", "d4_1")]
+        mn = [planes("mn0", "mn0", BF16), planes("mn1", "mn1", BF16)]
+        mg = sb.tile([P, S * PACK], BF16, name="mg", tag="tC", align_bytes=64)
+
+        def z2_gather(h, t):
+            nc.vector.tensor_tensor(d3[h][:, t, :], pick(hw[t], l3, h), hp[t][:, half(h)], ALU.subtract)
+            nc.vector.tensor_tensor(d4[h][:, t, :], pick(hw[t], l4, h), hp[t][:, half(h)], ALU.subtract)
+
+        def z2_min(h):
+            nc.vector.tensor_tensor(mn[h][:], d3[h][:], d4[h][:], ALU.min)
+            interleave(mg[:, h * HALF * PACK:(h + 1) * HALF * PACK], mn[h])
+
+        def z_first(t1, h):
+            for t in range(PACK):
+                nc.vector.tensor_tensor(t1[:, t, :], pick(ww[t], l1, h), hp[t][:, half(h)], ALU.subtract)
+
+        def z_second(t2, t1, h):
+            for t in range(PACK):
+                nc.vector.tensor_tensor(t2[:, t, :], pick(ww[t], l2, h), t1[:, t, :], ALU.add)
+
+        bb = [ps.tile([P, S], F32, name=f"b{t}", tag=f"bankB{t}") for t in range(PACK)]
+
+        for t in range(PACK):
+            z2_gather(0, t)
+        z2_gather(1, 0)
+        z2_min(0)
+        for t in range(1, PACK):
+            z2_gather(1, t)
+        z2_min(1)
+        nc.vector.quantize_mx(w2c[:].bitcast(X4), w2s[:], w2g[:])
+        t1 = planes("t1_0", "tA")
+        z_first(t1, 0)
+        second(bb, slice(0, S), *quantize("m", mg, S, "tB"))
+        bw, bp = [], []
+        for t in range(PACK):
+            a_ = sb.tile([P, S], F32, name=f"bw{t}")
+            b_ = sb.tile([P, S], F32, name=f"bp{t}")
+            nc.scalar.activation(a_[:], bb[t][:], ACT.Copy)
+            nc.scalar.activation(b_[:], bb[t][:], ACT.Copy)
+            bw.append(a_)
+            bp.append(b_)
+        t2 = planes("t2_0", "tC")
+        z_second(t2, t1, 0)
+        zg0 = sb.tile([P, HALF * PACK], BF16, name="zg0", tag="tD", align_bytes=64)
+        interleave(zg0[:], t2)
+        t1 = planes("t1_1", "tA")
+        z_first(t1, 1)
+        ab = [ps.tile([P, S], F32, name=f"a{t}", tag=f"bankA{t}") for t in range(PACK)]
+        aw = [sb.tile([P, S], F32, name=f"aw{t}") for t in range(PACK)]
+        second(ab, half(0), *quantize("z0", zg0, HALF, "z0c"))
+        for t in range(PACK):
+            nc.scalar.activation(aw[t][:, half(0)], ab[t][:, half(0)], ACT.Copy)
+        t2 = planes("t2_1", "tD")
+        z_second(t2, t1, 1)
+        zg1 = sb.tile([P, HALF * PACK], BF16, name="zg1", tag="tE", align_bytes=64)
+        interleave(zg1[:], t2)
+
+        sp, sm = [], []
+
+        def gate(db, t):
+            for h in range(2):
+                nc.vector.tensor_tensor(db[:, t % 2, half(h)], pick(bw[t], l6, h), bp[t][:, half(h)], ALU.subtract)
+            s_ = sb.tile([P, S], F32, name=f"sp{t}")
+            r_ = sb.tile([P, S], F32, name=f"sm{t}")
+            nc.scalar.activation(s_[:], db[:, t % 2, :], ACT.Sigmoid, scale=-1.0)
+            nc.scalar.activation(r_[:], s_[:], ACT.Copy, scale=-1.0, bias=1.0)
+            sp.append(s_)
+            sm.append(r_)
+
+        db = sb.tile([P, 2, S], F32, name="db01", tag="tA", align_bytes=64)
+        gate(db, 0)
+        gate(db, 1)
+        second(ab, half(1), *quantize("z1", zg1, HALF, "z1c"))
+        for t in range(PACK):
+            nc.scalar.activation(aw[t][:, half(1)], ab[t][:, half(1)], ACT.Copy)
+        db = sb.tile([P, 2, S], F32, name="db23", tag="tE", align_bytes=64)
+        gate(db, 2)
+        gate(db, 3)
+
+        outv = out.rearrange("(p t) j -> p t j", t=PACK)
+        pp = [sb.tile([P, S], F32, name=f"pp{t}") for t in range(PACK)]
+        qq = [sb.tile([P, S], F32, name=f"qq{t}") for t in range(PACK)]
+        oo = [sb.tile([P, S], F32, name=f"oo{t}") for t in range(PACK)]
+
+        def finish(t):
+            nc.vector.tensor_tensor(oo[t][:], qq[t][:], pp[t][:], ALU.add)
+            nc.sync.dma_start(outv[:, t, :], oo[t][:])
+
+        for t in range(PACK):
+            nc.vector.tensor_tensor(pp[t][:], ab[t][:], sm[t][:], ALU.mult)
+            nc.vector.tensor_tensor(qq[t][:, half(0)], pick(aw[t], l5, 0), sp[t][:, half(0)], ALU.mult)
+            if t > 0:
+                finish(t - 1)
+            nc.vector.tensor_tensor(qq[t][:, half(1)], pick(aw[t], l5, 1), sp[t][:, half(1)], ALU.mult)
+        finish(PACK - 1)

@@ -19,6 +19,9 @@ P = 128
 PACK = 4
 HALF = S // 2
 HCOL = HALF // 16
+ALL = slice(0, S)
+SPARE = slice(S, 2 * S)
+W1V = 72
 
 
 def tile_picked_tiepullblapunder_none_p_kernel(tc, x_words, x_scales, w1, gn, w2, offs, n1, n2, n3, n4, n5, n6, out):
@@ -39,11 +42,15 @@ def tile_picked_tiepullblapunder_none_p_kernel(tc, x_words, x_scales, w1, gn, w2
         def pick(window, lst, h):
             return window[:].indirect(lst[:, h * HCOL:(h + 1) * HCOL])
 
+        def f32(name, width=S, tag=None):
+            return sb.tile([P, width], F32, name=name, tag=tag or name, align_bytes=64)
+
         xs = sb.tile([P, T], U8, name="xs", align_bytes=64)
-        nc.vector.memset(xs[:].bitcast(I32), 0)
+        nc.gpsimd.memset(xs[:].bitcast(I32), 0)
         g = sb.tile([P, PACK], F32, name="g")
+        xst = sb.tile([P, T // 4], I32, name="xst")
         for q in range(4):
-            nc.scalar.dma_start(xs[32 * q:32 * q + 4, :].bitcast(I32), x_scales[0, 4 * q:4 * q + 4, :].bitcast(I32))
+            nc.scalar.dma_start(xst[32 * q:32 * q + 4, :], x_scales[0, 4 * q:4 * q + 4, :].bitcast(I32))
         w1r = sb.tile([P, PACK, H], F32, name="w1r", tag="wraw")
         nc.sync.dma_start(w1r[:], w1.rearrange("(p j) c -> p j c", j=PACK))
         lo = load_list("lo", offs)
@@ -57,6 +64,24 @@ def tile_picked_tiepullblapunder_none_p_kernel(tc, x_words, x_scales, w1, gn, w2
         l6 = load_list("l6", n6)
         l5 = load_list("l5", n5)
 
+        for q in range(4):
+            nc.vector.tensor_copy(xs[32 * q:32 * q + 4, :].bitcast(I32), xst[32 * q:32 * q + 4, :])
+        xsg = sb.tile([P, S], U8, name="xsg", align_bytes=64)
+        nc.vector.tensor_copy(xsg[:], xs[:].indirect(lo[:]))
+        w1g = sb.tile([P, PACK * H], BF16, name="w1g", align_bytes=64)
+        w1o = w1g[:].rearrange("p (t m j) -> p m j t", t=PACK, j=PACK)
+        w1i = w1r[:].rearrange("p j (m t) -> p m j t", t=PACK)
+        nc.vector.tensor_copy(w1o[:, 0:W1V], w1i[:, 0:W1V])
+        nc.scalar.copy(w1o[:, W1V:P], w1i[:, W1V:P])
+        w2r = sb.tile([P, PACK, H], F32, name="w2r", tag="wraw")
+        nc.sync.dma_start(w2r[:], w2.rearrange("(p j) c -> p j c", j=PACK))
+        w1c = sb.tile([P, H], U32, name="w1c", align_bytes=64)
+        w1s = sb.tile([P, H], U8, name="w1s", align_bytes=64)
+        nc.vector.quantize_mx(w1c[:].bitcast(X4), w1s[:], w1g[:])
+        xwg = [sb.tile([P, S], U32, name="xwg", align_bytes=64)]
+        for h in range(2):
+            nc.vector.tensor_copy(xwg[0][:, half(h)], pick(xw, lo, h))
+
         sg = sb.tile([P, PACK], F32, name="sg")
         sg2 = sb.tile([P, PACK], F32, name="sg2")
         ga = sb.tile([P, PACK], F32, name="ga")
@@ -68,42 +93,42 @@ def tile_picked_tiepullblapunder_none_p_kernel(tc, x_words, x_scales, w1, gn, w2
         nc.vector.tensor_tensor(ga[:], g[:], sg[:], ALU.mult)
         nc.vector.tensor_scalar(ga75[:], ga[:], 0.75, None, ALU.mult)
 
-        xsg = sb.tile([P, S], U8, name="xsg", align_bytes=64)
-        nc.vector.tensor_copy(xsg[:], xs[:].indirect(lo[:]))
-        w1g = sb.tile([P, PACK * H], BF16, name="w1g", align_bytes=64)
-        nc.vector.tensor_copy(w1g[:].rearrange("p (t m j) -> p m j t", t=PACK, j=PACK),
-                              w1r[:].rearrange("p j (m t) -> p m j t", t=PACK))
-        w2r = sb.tile([P, PACK, H], F32, name="w2r", tag="wraw")
-        nc.sync.dma_start(w2r[:], w2.rearrange("(p j) c -> p j c", j=PACK))
-        w1c = sb.tile([P, H], U32, name="w1c", align_bytes=64)
-        w1s = sb.tile([P, H], U8, name="w1s", align_bytes=64)
-        nc.vector.quantize_mx(w1c[:].bitcast(X4), w1s[:], w1g[:])
-        xwg = sb.tile([P, S], U32, name="xwg", align_bytes=64)
-        nc.vector.tensor_copy(xwg[:], xw[:].indirect(lo[:]))
-
-        yb = []
-        for t in range(PACK):
-            bank = ps.tile([P, S], F32, name=f"y{t}", tag=f"bankA{t}")
+        def product(bank, wc, ws, t, codes, scales):
             cols = slice(t * P, (t + 1) * P)
-            nc.tensor.matmul_mx(bank[:], lhsT=w1c[:, cols].bitcast(X4), lhsT_scale=w1s[:, cols],
-                                rhs=xwg[:].bitcast(X4), rhs_scale=xsg[:], start=True, stop=True)
-            yb.append(bank)
-        hw, hp, ww = [], [], []
-        for t in range(PACK):
-            a_ = sb.tile([P, S], F32, name=f"hw{t}")
-            b_ = sb.tile([P, S], F32, name=f"hp{t}")
-            nc.scalar.activation(a_[:], yb[t][:], ACT.Copy, scale=ga[:, t:t + 1])
-            nc.scalar.activation(b_[:], yb[t][:], ACT.Copy, scale=ga[:, t:t + 1])
-            hw.append(a_)
-            hp.append(b_)
-        for t in range(PACK):
-            c_ = sb.tile([P, S], F32, name=f"ww{t}")
-            nc.scalar.activation(c_[:], yb[t][:], ACT.Copy, scale=ga75[:, t:t + 1])
-            ww.append(c_)
+            nc.tensor.matmul_mx(bank, lhsT=wc[:, cols].bitcast(X4), lhsT_scale=ws[:, cols],
+                                rhs=codes.bitcast(X4), rhs_scale=scales, start=True, stop=True)
 
-        w2p = sb.tile([P, PACK, H], BF16, name="w2p")
+        y0 = [ps.tile([P, HALF], F32, name="y0_0", tag="bankA0"), ps.tile([P, HALF], F32, name="y0_1", tag="bankB0")]
+        for h in range(2):
+            product(y0[h][:], w1c, w1s, 0, xwg[0][:, half(h)], xsg[:, half(h)])
+        yb = [None]
+        for t in range(1, PACK):
+            bank = ps.tile([P, S], F32, name=f"y{t}", tag=f"bankA{t}")
+            product(bank[:], w1c, w1s, t, xwg[0][:], xsg[:])
+            yb.append(bank)
+        hw = [f32("hw0")] + [f32(f"hw{t}", 2 * S) for t in range(1, PACK)]
+        hp3 = f32("hp3")
+        hp = [hw[1][:, SPARE], hw[2][:, SPARE], hw[3][:, SPARE], hp3[:]]
+        ww = [f32(f"ww{t}") for t in range(PACK)]
+
+        def scaled(dst, src, factor, t):
+            nc.scalar.activation(dst, src, ACT.Copy, scale=factor[:, t:t + 1])
+
+        scaled(hw[0][:, half(0)], y0[0][:], ga, 0)
+        scaled(hp[0][:, half(0)], y0[0][:], ga, 0)
+        scaled(hw[0][:, half(1)], y0[1][:], ga, 0)
+        scaled(hp[0][:, half(1)], y0[1][:], ga, 0)
+        for t in range(1, PACK):
+            scaled(hw[t][:, ALL], yb[t][:], ga, t)
+            scaled(hp[t], yb[t][:], ga, t)
+        for h in range(2):
+            scaled(ww[0][:, half(h)], y0[h][:], ga75, 0)
+        for t in range(1, PACK):
+            scaled(ww[t][:], yb[t][:], ga75, t)
+
+        w2p = sb.tile([P, PACK, H], BF16, name="w2p", tag="tC", align_bytes=64)
         for j in range(PACK):
-            nc.scalar.activation(w2p[:, j, :], w2r[:, j, :], ACT.Copy, scale=sg[:, j:j + 1])
+            scaled(w2p[:, j, :], w2r[:, j, :], sg, j)
         w2g = sb.tile([P, PACK * H], BF16, name="w2g", tag="tB", align_bytes=64)
         nc.scalar.copy(w2g[:].rearrange("p (t m j) -> p m j t", t=PACK, j=PACK),
                        w2p[:].rearrange("p j (m t) -> p m j t", t=PACK))
@@ -112,7 +137,7 @@ def tile_picked_tiepullblapunder_none_p_kernel(tc, x_words, x_scales, w1, gn, w2
 
         def interleave(grp, planes):
             nc.scalar.copy(grp.rearrange("p (c i t) -> p c t i", i=4, t=PACK),
-                           planes[:].rearrange("p t (c i) -> p c t i", i=4))
+                           planes.rearrange("p t (c i) -> p c t i", i=4))
 
         def quantize(name, grp, width, tag):
             codes = sb.tile([P, width], U32, name=name + "c", tag=tag, align_bytes=64)
@@ -122,25 +147,29 @@ def tile_picked_tiepullblapunder_none_p_kernel(tc, x_words, x_scales, w1, gn, w2
 
         def second(banks, cs, codes, scales):
             for t in range(PACK):
-                cols = slice(t * P, (t + 1) * P)
-                nc.tensor.matmul_mx(banks[t][:, cs], lhsT=w2c[:, cols].bitcast(X4), lhsT_scale=w2s[:, cols],
-                                    rhs=codes[:].bitcast(X4), rhs_scale=scales[:], start=True, stop=True)
+                product(banks[t][:, cs], w2c, w2s, t, codes[:], scales[:])
 
-        def planes(name, tag, dt=F32):
-            return sb.tile([P, PACK, HALF], dt, name=name, tag=tag, align_bytes=64)
+        def planes(name, tag):
+            return sb.tile([P, PACK, HALF], F32, name=name, tag=tag, align_bytes=64)
 
-        d3 = [planes("d3_0", "d3_0"), planes("d3_1", "tA")]
-        d4 = [planes("d4_0", "d4_0"), planes("d4_1", "d4_1")]
-        mn = [planes("mn0", "mn0", BF16), planes("mn1", "mn1", BF16)]
+        d3 = [f32(f"d3_{t}") for t in range(PACK)]
+        d4 = [f32(f"d4_{t}", tag="tA" if t == 2 else None) for t in range(PACK)]
+        mn = sb.tile([P, PACK, S], BF16, name="mn", align_bytes=64)
         mg = sb.tile([P, S * PACK], BF16, name="mg", tag="tC", align_bytes=64)
 
-        def z2_gather(h, t):
-            nc.vector.tensor_tensor(d3[h][:, t, :], pick(hw[t], l3, h), hp[t][:, half(h)], ALU.subtract)
-            nc.vector.tensor_tensor(d4[h][:, t, :], pick(hw[t], l4, h), hp[t][:, half(h)], ALU.subtract)
+        def z2_min(t):
+            nc.vector.tensor_tensor(mn[:, t, :], d3[t][:], d4[t][:], ALU.min)
 
-        def z2_min(h):
-            nc.vector.tensor_tensor(mn[h][:], d3[h][:], d4[h][:], ALU.min)
-            interleave(mg[:, h * HALF * PACK:(h + 1) * HALF * PACK], mn[h])
+        for h in range(2):
+            nc.vector.tensor_tensor(d3[0][:, half(h)], pick(hw[0], l3, h), hp[0][:, half(h)], ALU.subtract)
+            nc.vector.tensor_tensor(d4[0][:, half(h)], pick(hw[0], l4, h), hp[0][:, half(h)], ALU.subtract)
+        for t in range(1, PACK):
+            nc.vector.tensor_tensor(d3[t][:], hw[t][:].indirect(l3[:]), hp[t], ALU.subtract)
+            z2_min(t - 1)
+            nc.vector.tensor_tensor(d4[t][:], hw[t][:].indirect(l4[:]), hp[t], ALU.subtract)
+        nc.vector.quantize_mx(w2c[:].bitcast(X4), w2s[:], w2g[:])
+        z2_min(PACK - 1)
+        interleave(mg[:], mn[:])
 
         def z_first(t1, h):
             for t in range(PACK):
@@ -151,53 +180,42 @@ def tile_picked_tiepullblapunder_none_p_kernel(tc, x_words, x_scales, w1, gn, w2
                 nc.vector.tensor_tensor(t2[:, t, :], pick(ww[t], l2, h), t1[:, t, :], ALU.add)
 
         bb = [ps.tile([P, S], F32, name=f"b{t}", tag=f"bankB{t}") for t in range(PACK)]
-
-        for t in range(PACK):
-            z2_gather(0, t)
-        z2_gather(1, 0)
-        z2_min(0)
-        for t in range(1, PACK):
-            z2_gather(1, t)
-        z2_min(1)
-        nc.vector.quantize_mx(w2c[:].bitcast(X4), w2s[:], w2g[:])
         t1 = planes("t1_0", "tA")
         z_first(t1, 0)
-        second(bb, slice(0, S), *quantize("m", mg, S, "tB"))
-        bw, bp = [], []
-        for t in range(PACK):
-            a_ = sb.tile([P, S], F32, name=f"bw{t}")
-            b_ = sb.tile([P, S], F32, name=f"bp{t}")
-            nc.scalar.activation(a_[:], bb[t][:], ACT.Copy)
-            nc.scalar.activation(b_[:], bb[t][:], ACT.Copy)
-            bw.append(a_)
-            bp.append(b_)
+        second(bb, ALL, *quantize("m", mg, S, "tB"))
+        bw = [f32(f"bw{t}", 2 * S) for t in range(PACK)]
+        bp = [bw[t ^ 1][:, SPARE] for t in range(PACK)]
+
+        def b_out(t):
+            nc.scalar.activation(bw[t][:, ALL], bb[t][:], ACT.Copy)
+            nc.scalar.activation(bp[t], bb[t][:], ACT.Copy)
+
+        b_out(0)
         t2 = planes("t2_0", "tC")
         z_second(t2, t1, 0)
         zg0 = sb.tile([P, HALF * PACK], BF16, name="zg0", tag="tD", align_bytes=64)
-        interleave(zg0[:], t2)
+        interleave(zg0[:], t2[:])
+        for t in range(1, PACK):
+            b_out(t)
         t1 = planes("t1_1", "tA")
         z_first(t1, 1)
         ab = [ps.tile([P, S], F32, name=f"a{t}", tag=f"bankA{t}") for t in range(PACK)]
-        aw = [sb.tile([P, S], F32, name=f"aw{t}") for t in range(PACK)]
+        aw = [f32(f"aw{t}", 2 * S) for t in range(PACK)]
         second(ab, half(0), *quantize("z0", zg0, HALF, "z0c"))
         for t in range(PACK):
             nc.scalar.activation(aw[t][:, half(0)], ab[t][:, half(0)], ACT.Copy)
         t2 = planes("t2_1", "tD")
         z_second(t2, t1, 1)
         zg1 = sb.tile([P, HALF * PACK], BF16, name="zg1", tag="tE", align_bytes=64)
-        interleave(zg1[:], t2)
+        interleave(zg1[:], t2[:])
 
-        sp, sm = [], []
+        sp = [f32(f"sp{t}") for t in range(PACK)]
+        sm = [aw[t][:, SPARE] for t in range(PACK)]
 
         def gate(db, t):
-            for h in range(2):
-                nc.vector.tensor_tensor(db[:, t % 2, half(h)], pick(bw[t], l6, h), bp[t][:, half(h)], ALU.subtract)
-            s_ = sb.tile([P, S], F32, name=f"sp{t}")
-            r_ = sb.tile([P, S], F32, name=f"sm{t}")
-            nc.scalar.activation(s_[:], db[:, t % 2, :], ACT.Sigmoid, scale=-1.0)
-            nc.scalar.activation(r_[:], s_[:], ACT.Copy, scale=-1.0, bias=1.0)
-            sp.append(s_)
-            sm.append(r_)
+            nc.vector.tensor_tensor(db[:, t % 2, :], bw[t][:].indirect(l6[:]), bp[t], ALU.subtract)
+            nc.scalar.activation(sp[t][:], db[:, t % 2, :], ACT.Sigmoid, scale=-1.0)
+            nc.scalar.activation(sm[t], sp[t][:], ACT.Copy, scale=-1.0, bias=1.0)
 
         db = sb.tile([P, 2, S], F32, name="db01", tag="tA", align_bytes=64)
         gate(db, 0)
@@ -210,18 +228,23 @@ def tile_picked_tiepullblapunder_none_p_kernel(tc, x_words, x_scales, w1, gn, w2
         gate(db, 3)
 
         outv = out.rearrange("(p t) j -> p t j", t=PACK)
-        pp = [sb.tile([P, S], F32, name=f"pp{t}") for t in range(PACK)]
-        qq = [sb.tile([P, S], F32, name=f"qq{t}") for t in range(PACK)]
-        oo = [sb.tile([P, S], F32, name=f"oo{t}") for t in range(PACK)]
+        pp = [f32(f"pp{t}") for t in range(PACK)]
+        qq = [f32(f"qq{t}") for t in range(PACK)]
+        oo = [f32(f"oo{t}") for t in range(PACK)]
 
-        def finish(t):
-            nc.vector.tensor_tensor(oo[t][:], qq[t][:], pp[t][:], ALU.add)
-            nc.sync.dma_start(outv[:, t, :], oo[t][:])
+        def finish(t, cs, queue):
+            nc.vector.tensor_tensor(oo[t][:, cs], qq[t][:, cs], pp[t][:, cs], ALU.add)
+            queue.dma_start(outv[:, t, cs], oo[t][:, cs])
 
-        for t in range(PACK):
-            nc.vector.tensor_tensor(pp[t][:], ab[t][:], sm[t][:], ALU.mult)
-            nc.vector.tensor_tensor(qq[t][:, half(0)], pick(aw[t], l5, 0), sp[t][:, half(0)], ALU.mult)
+        last = PACK - 1
+        for t in range(last):
+            nc.vector.tensor_tensor(pp[t][:], ab[t][:], sm[t], ALU.mult)
             if t > 0:
-                finish(t - 1)
-            nc.vector.tensor_tensor(qq[t][:, half(1)], pick(aw[t], l5, 1), sp[t][:, half(1)], ALU.mult)
-        finish(PACK - 1)
+                finish(t - 1, ALL, nc.sync)
+            nc.vector.tensor_tensor(qq[t][:], aw[t][:].indirect(l5[:]), sp[t][:], ALU.mult)
+        nc.vector.tensor_tensor(pp[last][:], ab[last][:], sm[last], ALU.mult)
+        nc.vector.tensor_tensor(qq[last][:, half(0)], pick(aw[last], l5, 0), sp[last][:, half(0)], ALU.mult)
+        finish(last - 1, ALL, nc.sync)
+        nc.vector.tensor_tensor(qq[last][:, half(1)], pick(aw[last], l5, 1), sp[last][:, half(1)], ALU.mult)
+        finish(last, half(0), nc.sync)
+        finish(last, half(1), nc.scalar)

@@ -49,14 +49,15 @@ def tile_picked_tiepullblapunder_none_p_kernel(tc, x_words, x_scales, w1, gn, w2
         nc.gpsimd.memset(xs[:].bitcast(I32), 0)
         g = sb.tile([P, PACK], F32, name="g")
         xst = sb.tile([P, T // 4], I32, name="xst")
+        nc.scalar.dma_start(g[:], gn.rearrange("(p t) o -> p (t o)", t=PACK))
+        lo = load_list("lo", offs)
         for q in range(4):
-            nc.scalar.dma_start(xst[32 * q:32 * q + 4, :], x_scales[0, 4 * q:4 * q + 4, :].bitcast(I32))
+            queue = nc.scalar if q < 2 else nc.sync
+            queue.dma_start(xst[32 * q:32 * q + 4, :], x_scales[0, 4 * q:4 * q + 4, :].bitcast(I32))
         w1r = sb.tile([P, PACK, H], F32, name="w1r", tag="wraw")
         nc.sync.dma_start(w1r[:], w1.rearrange("(p j) c -> p j c", j=PACK))
-        lo = load_list("lo", offs)
         xw = sb.tile([P, T], U32, name="xw", align_bytes=64)
         nc.sync.dma_start(xw[:].bitcast(I32), x_words[0].rearrange("p n r -> p (n r)").bitcast(I32))
-        nc.sync.dma_start(g[:], gn.rearrange("(p t) o -> p (t o)", t=PACK))
         l3 = load_list("l3", n3)
         l4 = load_list("l4", n4)
         l1 = load_list("l1", n1)
@@ -109,14 +110,14 @@ def tile_picked_tiepullblapunder_none_p_kernel(tc, x_words, x_scales, w1, gn, w2
         hw = [f32("hw0")] + [f32(f"hw{t}", 2 * S) for t in range(1, PACK)]
         hp3 = f32("hp3")
         hp = [hw[1][:, SPARE], hw[2][:, SPARE], hw[3][:, SPARE], hp3[:]]
-        ww = [f32(f"ww{t}") for t in range(PACK)]
+        ww = [f32(f"ww{t}", 2 * S) for t in range(PACK)]
 
         def scaled(dst, src, factor, t):
             nc.scalar.activation(dst, src, ACT.Copy, scale=factor[:, t:t + 1])
 
         scaled(hw[0][:, half(0)], y0[0][:], ga, 0)
-        scaled(hp[0][:, half(0)], y0[0][:], ga, 0)
         scaled(hw[0][:, half(1)], y0[1][:], ga, 0)
+        nc.vector.tensor_scalar(hp[0][:, half(0)], y0[0][:], ga[:, 0:1], None, ALU.mult)
         scaled(hp[0][:, half(1)], y0[1][:], ga, 0)
         for t in range(1, PACK):
             scaled(hw[t][:, ALL], yb[t][:], ga, t)
@@ -124,7 +125,7 @@ def tile_picked_tiepullblapunder_none_p_kernel(tc, x_words, x_scales, w1, gn, w2
         for h in range(2):
             scaled(ww[0][:, half(h)], y0[h][:], ga75, 0)
         for t in range(1, PACK):
-            scaled(ww[t][:], yb[t][:], ga75, t)
+            scaled(ww[t][:, ALL], yb[t][:], ga75, t)
 
         w2p = sb.tile([P, PACK, H], BF16, name="w2p", tag="tC", align_bytes=64)
         for j in range(PACK):
@@ -152,9 +153,9 @@ def tile_picked_tiepullblapunder_none_p_kernel(tc, x_words, x_scales, w1, gn, w2
         def planes(name, tag):
             return sb.tile([P, PACK, HALF], F32, name=name, tag=tag, align_bytes=64)
 
-        d3 = [f32(f"d3_{t}") for t in range(PACK)]
-        d4 = [f32(f"d4_{t}", tag="tA" if t == 2 else None) for t in range(PACK)]
-        mn = sb.tile([P, PACK, S], BF16, name="mn", align_bytes=64)
+        d3 = [ww[t][:, SPARE] for t in range(PACK)]
+        d4 = [f32(f"d4_{t}", tag=None) for t in range(PACK)]
+        mn = sb.tile([P, PACK, S], BF16, name="mn", tag="tD", align_bytes=64)
         mg = sb.tile([P, S * PACK], BF16, name="mg", tag="tC", align_bytes=64)
 
         def z2_min(t):
@@ -171,61 +172,43 @@ def tile_picked_tiepullblapunder_none_p_kernel(tc, x_words, x_scales, w1, gn, w2
         z2_min(PACK - 1)
         interleave(mg[:], mn[:])
 
-        def z_first(t1, h):
-            for t in range(PACK):
-                nc.vector.tensor_tensor(t1[:, t, :], pick(ww[t], l1, h), hp[t][:, half(h)], ALU.subtract)
-
-        def z_second(t2, t1, h):
-            for t in range(PACK):
-                nc.vector.tensor_tensor(t2[:, t, :], pick(ww[t], l2, h), t1[:, t, :], ALU.add)
-
         bb = [ps.tile([P, S], F32, name=f"b{t}", tag=f"bankB{t}") for t in range(PACK)]
-        t1 = planes("t1_0", "tA")
-        z_first(t1, 0)
-        second(bb, ALL, *quantize("m", mg, S, "tB"))
+        t1 = [f32(f"t1_{t}")[:] for t in range(PACK - 1)]
+        for t in range(PACK - 1):
+            nc.vector.tensor_tensor(t1[t], ww[t][:].indirect(l1[:]), hp[t], ALU.subtract)
+        second(bb, ALL, *quantize("m", mg, S, "mc"))
         bw = [f32(f"bw{t}", 2 * S) for t in range(PACK)]
         bp = [bw[t ^ 1][:, SPARE] for t in range(PACK)]
-
-        def b_out(t):
+        for t in range(PACK):
             nc.scalar.activation(bw[t][:, ALL], bb[t][:], ACT.Copy)
-            nc.scalar.activation(bp[t], bb[t][:], ACT.Copy)
+            nc.sync.dma_start(bp[t], bw[t][:, ALL])
+        late = f32("late", (1 + PACK) * S, "tC")
+        t1.append(late[:, PACK * S:])
+        nc.vector.tensor_tensor(t1[3], ww[3][:].indirect(l1[:]), hp[3], ALU.subtract)
+        zg = sb.tile([P, S * PACK], BF16, name="zg", tag="tD", align_bytes=64)
+        for h in range(2):
+            t2 = late[:, h * PACK * HALF:(h + 1) * PACK * HALF].rearrange("p (t j) -> p t j", t=PACK)
+            for t in range(PACK):
+                nc.vector.tensor_tensor(t2[:, t, :], pick(ww[t], l2, h), t1[t][:, half(h)], ALU.add)
+            interleave(zg[:, h * PACK * HALF:(h + 1) * PACK * HALF], t2)
 
-        b_out(0)
-        t2 = planes("t2_0", "tC")
-        z_second(t2, t1, 0)
-        zg0 = sb.tile([P, HALF * PACK], BF16, name="zg0", tag="tD", align_bytes=64)
-        interleave(zg0[:], t2[:])
-        for t in range(1, PACK):
-            b_out(t)
-        t1 = planes("t1_1", "tA")
-        z_first(t1, 1)
         ab = [ps.tile([P, S], F32, name=f"a{t}", tag=f"bankA{t}") for t in range(PACK)]
         aw = [f32(f"aw{t}", 2 * S) for t in range(PACK)]
-        second(ab, half(0), *quantize("z0", zg0, HALF, "z0c"))
-        for t in range(PACK):
-            nc.scalar.activation(aw[t][:, half(0)], ab[t][:, half(0)], ACT.Copy)
-        t2 = planes("t2_1", "tD")
-        z_second(t2, t1, 1)
-        zg1 = sb.tile([P, HALF * PACK], BF16, name="zg1", tag="tE", align_bytes=64)
-        interleave(zg1[:], t2[:])
-
-        sp = [f32(f"sp{t}") for t in range(PACK)]
-        sm = [aw[t][:, SPARE] for t in range(PACK)]
+        sp = [aw[t ^ 1][:, SPARE] for t in range(PACK)]
 
         def gate(db, t):
             nc.vector.tensor_tensor(db[:, t % 2, :], bw[t][:].indirect(l6[:]), bp[t], ALU.subtract)
-            nc.scalar.activation(sp[t][:], db[:, t % 2, :], ACT.Sigmoid, scale=-1.0)
-            nc.scalar.activation(sm[t], sp[t][:], ACT.Copy, scale=-1.0, bias=1.0)
+            nc.scalar.activation(sp[t], db[:, t % 2, :], ACT.Sigmoid, scale=-1.0)
 
-        db = sb.tile([P, 2, S], F32, name="db01", tag="tA", align_bytes=64)
+        db = sb.tile([P, 2, S], F32, name="db01", align_bytes=64)
         gate(db, 0)
         gate(db, 1)
-        second(ab, half(1), *quantize("z1", zg1, HALF, "z1c"))
+        second(ab, ALL, *quantize("z", zg, S, "bw0"))
+        db = sb.tile([P, 2, S], F32, name="db23", tag="tD", align_bytes=64)
         for t in range(PACK):
-            nc.scalar.activation(aw[t][:, half(1)], ab[t][:, half(1)], ACT.Copy)
-        db = sb.tile([P, 2, S], F32, name="db23", tag="tE", align_bytes=64)
-        gate(db, 2)
-        gate(db, 3)
+            nc.scalar.activation(aw[t][:, ALL], ab[t][:], ACT.Copy)
+            if t < 2:
+                gate(db, t + 2)
 
         outv = out.rearrange("(p t) j -> p t j", t=PACK)
         pp = [f32(f"pp{t}") for t in range(PACK)]
@@ -233,16 +216,16 @@ def tile_picked_tiepullblapunder_none_p_kernel(tc, x_words, x_scales, w1, gn, w2
         oo = [f32(f"oo{t}") for t in range(PACK)]
 
         def finish(t, cs, queue):
-            nc.vector.tensor_tensor(oo[t][:, cs], qq[t][:, cs], pp[t][:, cs], ALU.add)
+            nc.vector.tensor_tensor(oo[t][:, cs], qq[t][:, cs], pp[t][:, cs], ALU.subtract)
             queue.dma_start(outv[:, t, cs], oo[t][:, cs])
 
         last = PACK - 1
         for t in range(last):
-            nc.vector.tensor_tensor(pp[t][:], ab[t][:], sm[t], ALU.mult)
+            nc.vector.scalar_tensor_tensor(pp[t][:], sp[t], 1.0, ab[t][:], ALU.subtract, ALU.mult)
             if t > 0:
                 finish(t - 1, ALL, nc.sync)
-            nc.vector.tensor_tensor(qq[t][:], aw[t][:].indirect(l5[:]), sp[t][:], ALU.mult)
-        nc.vector.tensor_tensor(pp[last][:], ab[last][:], sm[last], ALU.mult)
+            nc.vector.tensor_tensor(qq[t][:], aw[t][:].indirect(l5[:]), sp[t], ALU.mult)
+        nc.vector.scalar_tensor_tensor(pp[last][:], sp[last], 1.0, ab[last][:], ALU.subtract, ALU.mult)
         nc.vector.tensor_tensor(qq[last][:, half(0)], pick(aw[last], l5, 0), sp[last][:, half(0)], ALU.mult)
         finish(last - 1, ALL, nc.sync)
         nc.vector.tensor_tensor(qq[last][:, half(1)], pick(aw[last], l5, 1), sp[last][:, half(1)], ALU.mult)

@@ -1,8 +1,9 @@
 from contextlib import ExitStack
 
 import concourse.mybir as mybir
+from concourse.masks import make_identity
 
-K, T, S, H = 512, 2048, 512, 512
+T, S, H = 2048, 512, 512
 FLOPS = 3 * 2 * 512 * 512 * 512
 
 F32 = mybir.dt.float32
@@ -17,11 +18,13 @@ ACT = mybir.ActivationFunctionType
 
 P = 128
 PACK = 4
+LAST = PACK - 1
 HALF = S // 2
-HCOL = HALF // 16
-ALL = slice(0, S)
+HALF_COLS = HALF // 16
+PLANE = slice(0, S)
 SPARE = slice(S, 2 * S)
-W1V = 72
+W1_ON_VECTOR = 64
+TURNED = 2
 
 
 def tile_picked_tiepullblapunder_none_p_kernel(tc, x_words, x_scales, w1, gn, w2, offs, n1, n2, n3, n4, n5, n6, out):
@@ -32,202 +35,249 @@ def tile_picked_tiepullblapunder_none_p_kernel(tc, x_words, x_scales, w1, gn, w2
         ps = ctx.enter_context(tc.psum_pool(name="ps", bufs=1))
 
         def load_list(name, src):
-            tl = lists.tile([P, S // 16], U16, name=name)
-            nc.sync.dma_start(tl[:], src)
-            return tl
+            offsets = lists.tile([P, S // 16], U16, name=name)
+            nc.sync.dma_start(offsets[:], src)
+            return offsets
 
         def half(h):
             return slice(h * HALF, (h + 1) * HALF)
 
-        def pick(window, lst, h):
-            return window[:].indirect(lst[:, h * HCOL:(h + 1) * HCOL])
+        def half_words(h):
+            return slice(h * HALF * PACK, (h + 1) * HALF * PACK)
+
+        def plane(t):
+            return slice(t * S, (t + 1) * S)
+
+        def pick(window, offsets):
+            return window[:].indirect(offsets[:])
+
+        def pick_half(window, offsets, h):
+            return window[:].indirect(offsets[:, h * HALF_COLS:(h + 1) * HALF_COLS])
+
+        def tile(name, width, dtype, tag=None):
+            return sb.tile([P, width], dtype, name=name, tag=tag or name, align_bytes=64)
 
         def f32(name, width=S, tag=None):
-            return sb.tile([P, width], F32, name=name, tag=tag or name, align_bytes=64)
+            return tile(name, width, F32, tag)
 
-        xs = sb.tile([P, T], U8, name="xs", align_bytes=64)
-        nc.gpsimd.memset(xs[:].bitcast(I32), 0)
-        g = sb.tile([P, PACK], F32, name="g")
-        xst = sb.tile([P, T // 4], I32, name="xst")
-        nc.scalar.dma_start(g[:], gn.rearrange("(p t) o -> p (t o)", t=PACK))
-        lo = load_list("lo", offs)
-        for q in range(4):
-            queue = nc.scalar if q < 2 else nc.sync
-            queue.dma_start(xst[32 * q:32 * q + 4, :], x_scales[0, 4 * q:4 * q + 4, :].bitcast(I32))
-        w1r = sb.tile([P, PACK, H], F32, name="w1r", tag="wraw")
-        nc.sync.dma_start(w1r[:], w1.rearrange("(p j) c -> p j c", j=PACK))
-        xw = sb.tile([P, T], U32, name="xw", align_bytes=64)
-        nc.sync.dma_start(xw[:].bitcast(I32), x_words[0].rearrange("p n r -> p (n r)").bitcast(I32))
-        l3 = load_list("l3", n3)
-        l4 = load_list("l4", n4)
-        l1 = load_list("l1", n1)
-        l2 = load_list("l2", n2)
-        l6 = load_list("l6", n6)
-        l5 = load_list("l5", n5)
+        def bank(name, width, tag):
+            return ps.tile([P, width], F32, name=name, tag=tag)
 
-        for q in range(4):
-            nc.vector.tensor_copy(xs[32 * q:32 * q + 4, :].bitcast(I32), xst[32 * q:32 * q + 4, :])
-        xsg = sb.tile([P, S], U8, name="xsg", align_bytes=64)
-        nc.vector.tensor_copy(xsg[:], xs[:].indirect(lo[:]))
-        w1g = sb.tile([P, PACK * H], BF16, name="w1g", align_bytes=64)
-        w1o = w1g[:].rearrange("p (t m j) -> p m j t", t=PACK, j=PACK)
-        w1i = w1r[:].rearrange("p j (m t) -> p m j t", t=PACK)
-        nc.vector.tensor_copy(w1o[:, 0:W1V], w1i[:, 0:W1V])
-        nc.scalar.copy(w1o[:, W1V:P], w1i[:, W1V:P])
-        w2r = sb.tile([P, PACK, H], F32, name="w2r", tag="wraw")
-        nc.sync.dma_start(w2r[:], w2.rearrange("(p j) c -> p j c", j=PACK))
-        w1c = sb.tile([P, H], U32, name="w1c", align_bytes=64)
-        w1s = sb.tile([P, H], U8, name="w1s", align_bytes=64)
-        nc.vector.quantize_mx(w1c[:].bitcast(X4), w1s[:], w1g[:])
-        xwg = [sb.tile([P, S], U32, name="xwg", align_bytes=64)]
-        for h in range(2):
-            nc.vector.tensor_copy(xwg[0][:, half(h)], pick(xw, lo, h))
-
-        sg = sb.tile([P, PACK], F32, name="sg")
-        sg2 = sb.tile([P, PACK], F32, name="sg2")
-        ga = sb.tile([P, PACK], F32, name="ga")
-        ga75 = sb.tile([P, PACK], F32, name="ga75")
-        warm = sb.tile([P, PACK], F32, name="warm")
-        nc.scalar.activation(warm[:], g[:], ACT.Sigmoid)
-        nc.vector.tensor_scalar(sg2[:], g[:], 0.0, 2.0, ALU.is_ge, ALU.mult)
-        nc.vector.tensor_scalar(sg[:], sg2[:], -1.0, None, ALU.add)
-        nc.vector.tensor_tensor(ga[:], g[:], sg[:], ALU.mult)
-        nc.vector.tensor_scalar(ga75[:], ga[:], 0.75, None, ALU.mult)
-
-        def product(bank, wc, ws, t, codes, scales):
+        def product(dst, w_codes, w_scales, t, codes, scales):
             cols = slice(t * P, (t + 1) * P)
-            nc.tensor.matmul_mx(bank, lhsT=wc[:, cols].bitcast(X4), lhsT_scale=ws[:, cols],
+            nc.tensor.matmul_mx(dst, lhsT=w_codes[:, cols].bitcast(X4), lhsT_scale=w_scales[:, cols],
                                 rhs=codes.bitcast(X4), rhs_scale=scales, start=True, stop=True)
-
-        y0 = [ps.tile([P, HALF], F32, name="y0_0", tag="bankA0"), ps.tile([P, HALF], F32, name="y0_1", tag="bankB0")]
-        for h in range(2):
-            product(y0[h][:], w1c, w1s, 0, xwg[0][:, half(h)], xsg[:, half(h)])
-        yb = [None]
-        for t in range(1, PACK):
-            bank = ps.tile([P, S], F32, name=f"y{t}", tag=f"bankA{t}")
-            product(bank[:], w1c, w1s, t, xwg[0][:], xsg[:])
-            yb.append(bank)
-        hw = [f32("hw0")] + [f32(f"hw{t}", 2 * S) for t in range(1, PACK)]
-        hp3 = f32("hp3")
-        hp = [hw[1][:, SPARE], hw[2][:, SPARE], hw[3][:, SPARE], hp3[:]]
-        ww = [f32(f"ww{t}", 2 * S) for t in range(PACK)]
 
         def scaled(dst, src, factor, t):
             nc.scalar.activation(dst, src, ACT.Copy, scale=factor[:, t:t + 1])
 
-        scaled(hw[0][:, half(0)], y0[0][:], ga, 0)
-        scaled(hw[0][:, half(1)], y0[1][:], ga, 0)
-        nc.vector.tensor_scalar(hp[0][:, half(0)], y0[0][:], ga[:, 0:1], None, ALU.mult)
-        scaled(hp[0][:, half(1)], y0[1][:], ga, 0)
-        for t in range(1, PACK):
-            scaled(hw[t][:, ALL], yb[t][:], ga, t)
-            scaled(hp[t], yb[t][:], ga, t)
-        for h in range(2):
-            scaled(ww[0][:, half(h)], y0[h][:], ga75, 0)
-        for t in range(1, PACK):
-            scaled(ww[t][:, ALL], yb[t][:], ga75, t)
+        def words_view(words):
+            return words.rearrange("p (c i t) -> p c t i", i=4, t=PACK)
 
-        w2p = sb.tile([P, PACK, H], BF16, name="w2p", tag="tC", align_bytes=64)
+        def planes_view(planes):
+            return planes.rearrange("p (t c i) -> p c t i", i=4, t=PACK)
+
+        x_scale_table = tile("x_scale_table", T, U8)
+        nc.gpsimd.memset(x_scale_table[:].bitcast(I32), 0)
+        gain = f32("gain", PACK)
+        x_scale_rows = tile("x_scale_rows", T // 4, I32)
+        nc.scalar.dma_start(gain[:], gn.rearrange("(p t) o -> p (t o)", t=PACK))
+        idx = load_list("idx", offs)
+        for q in range(4):
+            queue = nc.scalar if q < 2 else nc.sync
+            queue.dma_start(x_scale_rows[32 * q:32 * q + 4, :], x_scales[0, 4 * q:4 * q + 4, :].bitcast(I32))
+        w1_raw = sb.tile([P, PACK, H], F32, name="w1_raw", tag="w_raw", align_bytes=64)
+        nc.sync.dma_start(w1_raw[:], w1.rearrange("(p j) c -> p j c", j=PACK))
+        x_word_table = tile("x_word_table", T, U32)
+        nc.sync.dma_start(x_word_table[:].bitcast(I32), x_words[0].rearrange("p n r -> p (n r)").bitcast(I32))
+        list3 = load_list("list3", n3)
+        list4 = load_list("list4", n4)
+        list1 = load_list("list1", n1)
+        list2 = load_list("list2", n2)
+        list6 = load_list("list6", n6)
+        list5 = load_list("list5", n5)
+
+        gain_step2, gain_sign, gain_abs, gain_abs75 = (f32(n, PACK) for n in ("gain_step2", "gain_sign", "gain_abs", "gain_abs75"))
+        nc.scalar.activation(gain_abs[:], gain[:], ACT.Abs)
+        nc.scalar.activation(gain_abs75[:], gain[:], ACT.Abs, scale=0.75)
+        nc.gpsimd.tensor_scalar(gain_step2[:], gain[:], 0.0, 2.0, ALU.is_ge, ALU.mult)
+        nc.gpsimd.tensor_scalar(gain_sign[:], gain_step2[:], -1.0, None, ALU.add)
+        ident = f32("ident", P)
+        make_identity(nc, ident[:])
+
+        for q in range(4):
+            nc.vector.tensor_copy(x_scale_table[32 * q:32 * q + 4, :].bitcast(I32), x_scale_rows[32 * q:32 * q + 4, :])
+        x_picked_scales = tile("x_picked_scales", S, U8)
+        nc.vector.tensor_copy(x_picked_scales[:], pick(x_scale_table, idx))
+        w1_bf = tile("w1_bf", PACK * H, BF16)
+        w1_to = w1_bf[:].rearrange("p (t m j) -> p m j t", t=PACK, j=PACK)
+        w1_from = w1_raw[:].rearrange("p j (m t) -> p m j t", t=PACK)
+        nc.vector.tensor_copy(w1_to[:, 0:W1_ON_VECTOR], w1_from[:, 0:W1_ON_VECTOR])
+        nc.scalar.copy(w1_to[:, W1_ON_VECTOR:P], w1_from[:, W1_ON_VECTOR:P])
+        w2_raw = sb.tile([P, PACK, H], F32, name="w2_raw", tag="w_raw", align_bytes=64)
+        nc.sync.dma_start(w2_raw[:], w2.rearrange("(p j) c -> p j c", j=PACK))
+        w1_codes = tile("w1_codes", H, U32)
+        w1_scales = tile("w1_scales", H, U8)
+        nc.vector.quantize_mx(w1_codes[:].bitcast(X4), w1_scales[:], w1_bf[:])
+        x_picked_words = tile("x_picked_words", S, U32, "w1_bf")
+        for h in range(2):
+            nc.vector.tensor_copy(x_picked_words[:, half(h)], pick_half(x_word_table, idx, h))
+
+        y0_banks = [bank("y0_0", HALF, "bankA0"), bank("y0_1", HALF, "bankB0")]
+        for h in range(2):
+            product(y0_banks[h][:], w1_codes, w1_scales, 0, x_picked_words[:, half(h)], x_picked_scales[:, half(h)])
+        y_banks = {}
+        for t in range(1, PACK):
+            y_banks[t] = bank(f"y{t}", S, f"bankA{t}")
+            product(y_banks[t][:], w1_codes, w1_scales, t, x_picked_words[:], x_picked_scales[:])
+
+        h_win = [f32("h_win0")] + [f32(f"h_win{t}", 2 * S) for t in range(1, PACK)]
+        h75_win = [f32(f"h75_win{t}", 2 * S) for t in range(PACK)]
+        b_win = [f32(f"b_win{t}", 2 * S) for t in range(PACK)]
+        h_plain = [h_win[1][:, SPARE], h_win[2][:, SPARE], h75_win[1][:, SPARE], h75_win[0][:, SPARE]]
+        for window in (h_win[3], h75_win[2], h75_win[3]):
+            nc.vector.memset(window[:, SPARE], 0.0)
+
+        scaled(h_win[0][:, half(0)], y0_banks[0][:], gain_abs, 0)
+        scaled(h_win[0][:, half(1)], y0_banks[1][:], gain_abs, 0)
+        nc.vector.tensor_scalar(h_plain[0][:, half(0)], y0_banks[0][:], gain_abs[:, 0:1], None, ALU.mult)
+        scaled(h_plain[0][:, half(1)], y0_banks[1][:], gain_abs, 0)
+        scaled(h_win[1][:, PLANE], y_banks[1][:], gain_abs, 1)
+        scaled(h_plain[1], y_banks[1][:], gain_abs, 1)
+        for t in range(2, PACK):
+            scaled(h_win[t][:, PLANE], y_banks[t][:], gain_abs, t)
+            nc.sync.dma_start(h_plain[t], h_win[t][:, PLANE])
+        for h in range(2):
+            scaled(h75_win[0][:, half(h)], y0_banks[h][:], gain_abs75, 0)
+        for t in range(1, LAST):
+            scaled(h75_win[t][:, PLANE], y_banks[t][:], gain_abs75, t)
+
+        w2_signed = tile("w2_signed", PACK * H, BF16)
         for j in range(PACK):
-            scaled(w2p[:, j, :], w2r[:, j, :], sg, j)
-        w2g = sb.tile([P, PACK * H], BF16, name="w2g", tag="tB", align_bytes=64)
-        nc.scalar.copy(w2g[:].rearrange("p (t m j) -> p m j t", t=PACK, j=PACK),
-                       w2p[:].rearrange("p j (m t) -> p m j t", t=PACK))
-        w2c = sb.tile([P, H], U32, name="w2c", align_bytes=64)
-        w2s = sb.tile([P, H], U8, name="w2s", align_bytes=64)
+            scaled(w2_signed[:, j * H:(j + 1) * H], w2_raw[:, j, :], gain_sign, j)
+        scaled(h75_win[LAST][:, PLANE], y_banks[LAST][:], gain_abs75, LAST)
+        w2_bf = tile("w2_bf", PACK * H, BF16)
+        nc.scalar.copy(w2_bf[:].rearrange("p (t m j) -> p m j t", t=PACK, j=PACK),
+                       w2_signed[:].rearrange("p (j m t) -> p m j t", j=PACK, t=PACK))
 
-        def interleave(grp, planes):
-            nc.scalar.copy(grp.rearrange("p (c i t) -> p c t i", i=4, t=PACK),
-                           planes.rearrange("p t (c i) -> p c t i", i=4))
-
-        def quantize(name, grp, width, tag):
-            codes = sb.tile([P, width], U32, name=name + "c", tag=tag, align_bytes=64)
-            scales = sb.tile([P, width], U8, name=name + "s", align_bytes=64)
-            nc.vector.quantize_mx(codes[:].bitcast(X4), scales[:], grp[:])
-            return codes, scales
-
-        def second(banks, cs, codes, scales):
-            for t in range(PACK):
-                product(banks[t][:, cs], w2c, w2s, t, codes[:], scales[:])
-
-        def planes(name, tag):
-            return sb.tile([P, PACK, HALF], F32, name=name, tag=tag, align_bytes=64)
-
-        d3 = [ww[t][:, SPARE] for t in range(PACK)]
-        d4 = [f32(f"d4_{t}", tag=None) for t in range(PACK)]
-        mn = sb.tile([P, PACK, S], BF16, name="mn", tag="tD", align_bytes=64)
-        mg = sb.tile([P, S * PACK], BF16, name="mg", tag="tC", align_bytes=64)
-
-        def z2_min(t):
-            nc.vector.tensor_tensor(mn[:, t, :], d3[t][:], d4[t][:], ALU.min)
-
+        diff3 = f32("diff3", PACK * S)
+        diff4 = f32("diff4", PACK * S)
         for h in range(2):
-            nc.vector.tensor_tensor(d3[0][:, half(h)], pick(hw[0], l3, h), hp[0][:, half(h)], ALU.subtract)
-            nc.vector.tensor_tensor(d4[0][:, half(h)], pick(hw[0], l4, h), hp[0][:, half(h)], ALU.subtract)
+            nc.vector.tensor_tensor(diff3[:, half(h)], pick_half(h_win[0], list3, h), h_plain[0][:, half(h)], ALU.subtract)
+            nc.vector.tensor_tensor(diff4[:, half(h)], pick_half(h_win[0], list4, h), h_plain[0][:, half(h)], ALU.subtract)
         for t in range(1, PACK):
-            nc.vector.tensor_tensor(d3[t][:], hw[t][:].indirect(l3[:]), hp[t], ALU.subtract)
-            z2_min(t - 1)
-            nc.vector.tensor_tensor(d4[t][:], hw[t][:].indirect(l4[:]), hp[t], ALU.subtract)
-        nc.vector.quantize_mx(w2c[:].bitcast(X4), w2s[:], w2g[:])
-        z2_min(PACK - 1)
-        interleave(mg[:], mn[:])
-
-        bb = [ps.tile([P, S], F32, name=f"b{t}", tag=f"bankB{t}") for t in range(PACK)]
-        t1 = [f32(f"t1_{t}")[:] for t in range(PACK - 1)]
-        for t in range(PACK - 1):
-            nc.vector.tensor_tensor(t1[t], ww[t][:].indirect(l1[:]), hp[t], ALU.subtract)
-        second(bb, ALL, *quantize("m", mg, S, "mc"))
-        bw = [f32(f"bw{t}", 2 * S) for t in range(PACK)]
-        bp = [bw[t ^ 1][:, SPARE] for t in range(PACK)]
-        for t in range(PACK):
-            nc.scalar.activation(bw[t][:, ALL], bb[t][:], ACT.Copy)
-            nc.sync.dma_start(bp[t], bw[t][:, ALL])
-        late = f32("late", (1 + PACK) * S, "tC")
-        t1.append(late[:, PACK * S:])
-        nc.vector.tensor_tensor(t1[3], ww[3][:].indirect(l1[:]), hp[3], ALU.subtract)
-        zg = sb.tile([P, S * PACK], BF16, name="zg", tag="tD", align_bytes=64)
+            nc.vector.tensor_tensor(diff3[:, plane(t)], pick(h_win[t], list3), h_plain[t], ALU.subtract)
+            nc.vector.tensor_tensor(diff4[:, plane(t)], pick(h_win[t], list4), h_plain[t], ALU.subtract)
+        diff3_bf = tile("diff3_bf", PACK * S, BF16, "w_raw")
+        nc.scalar.copy(words_view(diff3_bf[:]), planes_view(diff3[:]))
+        diff4_bf = [tile("diff4_bf0", PACK * HALF, BF16, "w2_signed"),
+                    tile("diff4_bf1", PACK * HALF, BF16, "diff3")]
         for h in range(2):
-            t2 = late[:, h * PACK * HALF:(h + 1) * PACK * HALF].rearrange("p (t j) -> p t j", t=PACK)
-            for t in range(PACK):
-                nc.vector.tensor_tensor(t2[:, t, :], pick(ww[t], l2, h), t1[t][:, half(h)], ALU.add)
-            interleave(zg[:, h * PACK * HALF:(h + 1) * PACK * HALF], t2)
+            nc.scalar.copy(words_view(diff4_bf[h][:]), planes_view(diff4[:])[:, h * HALF // 4:(h + 1) * HALF // 4])
+        min_bf = tile("min_bf", PACK * S, BF16)
 
-        ab = [ps.tile([P, S], F32, name=f"a{t}", tag=f"bankA{t}") for t in range(PACK)]
-        aw = [f32(f"aw{t}", 2 * S) for t in range(PACK)]
-        sp = [aw[t ^ 1][:, SPARE] for t in range(PACK)]
-
-        def gate(db, t):
-            nc.vector.tensor_tensor(db[:, t % 2, :], bw[t][:].indirect(l6[:]), bp[t], ALU.subtract)
-            nc.scalar.activation(sp[t], db[:, t % 2, :], ACT.Sigmoid, scale=-1.0)
-
-        db = sb.tile([P, 2, S], F32, name="db01", align_bytes=64)
-        gate(db, 0)
-        gate(db, 1)
-        second(ab, ALL, *quantize("z", zg, S, "bw0"))
-        db = sb.tile([P, 2, S], F32, name="db23", tag="tD", align_bytes=64)
+        part_rest = f32("part_rest", LAST * S, f"h_win{LAST}")
+        part = [b_win[0][:, SPARE]] + [part_rest[:, plane(t)] for t in range(LAST)]
         for t in range(PACK):
-            nc.scalar.activation(aw[t][:, ALL], ab[t][:], ACT.Copy)
-            if t < 2:
-                gate(db, t + 2)
+            nc.vector.tensor_tensor(part[t], pick(h75_win[t], list1), h_plain[t], ALU.subtract)
 
-        outv = out.rearrange("(p t) j -> p t j", t=PACK)
-        pp = [f32(f"pp{t}") for t in range(PACK)]
-        qq = [f32(f"qq{t}") for t in range(PACK)]
-        oo = [f32(f"oo{t}") for t in range(PACK)]
+        min_codes = tile("min_codes", S, U32)
+        min_scales = tile("min_scales", S, U8)
+        for h in range(2):
+            nc.vector.tensor_tensor(min_bf[:, half_words(h)], diff3_bf[:, half_words(h)], diff4_bf[h][:], ALU.min)
+        w2_codes = tile("w2_codes", H, U32, "diff4")
+        w2_scales = tile("w2_scales", H, U8)
+        nc.vector.quantize_mx(w2_codes[:].bitcast(X4), w2_scales[:], w2_bf[:])
+        nc.vector.quantize_mx(min_codes[:].bitcast(X4), min_scales[:], min_bf[:])
+        b_banks = [bank(f"b{t}", S, f"bankB{t}") for t in range(PACK)]
+        for t in range(PACK):
+            product(b_banks[t][:], w2_codes, w2_scales, t, min_codes[:], min_scales[:])
+        b_plain = [b_win[t + 1][:, SPARE] for t in range(LAST)] + [f32("b_plain_last")[:]]
+        for t in range(PACK):
+            nc.scalar.activation(b_win[t][:, PLANE], b_banks[t][:], ACT.Copy)
+            nc.sync.dma_start(b_plain[t], b_win[t][:, PLANE])
 
-        def finish(t, cs, queue):
-            nc.vector.tensor_tensor(oo[t][:, cs], qq[t][:, cs], pp[t][:, cs], ALU.subtract)
-            queue.dma_start(outv[:, t, cs], oo[t][:, cs])
+        z_f32 = f32("z_f32", PACK * S, "diff3")
+        z_bf = tile("z_bf", PACK * S, BF16)
+        for h in range(2):
+            for t in range(PACK):
+                at = (h * PACK + t) * HALF
+                nc.vector.tensor_tensor(z_f32[:, at:at + HALF], pick_half(h75_win[t], list2, h), part[t][:, half(h)], ALU.add)
+            nc.scalar.copy(words_view(z_bf[:, half_words(h)]), planes_view(z_f32[:, half_words(h)]))
 
-        last = PACK - 1
-        for t in range(last):
-            nc.vector.scalar_tensor_tensor(pp[t][:], sp[t], 1.0, ab[t][:], ALU.subtract, ALU.mult)
-            if t > 0:
-                finish(t - 1, ALL, nc.sync)
-            nc.vector.tensor_tensor(qq[t][:], aw[t][:].indirect(l5[:]), sp[t], ALU.mult)
-        nc.vector.scalar_tensor_tensor(pp[last][:], sp[last], 1.0, ab[last][:], ALU.subtract, ALU.mult)
-        nc.vector.tensor_tensor(qq[last][:, half(0)], pick(aw[last], l5, 0), sp[last][:, half(0)], ALU.mult)
-        finish(last - 1, ALL, nc.sync)
-        nc.vector.tensor_tensor(qq[last][:, half(1)], pick(aw[last], l5, 1), sp[last][:, half(1)], ALU.mult)
-        finish(last, half(0), nc.sync)
-        finish(last, half(1), nc.scalar)
+        a_banks = [bank(f"a{t}", S, f"bankA{t}") for t in range(PACK)]
+        a_win = [f32("a_win0", 2 * S), f32("a_win1", 2 * S)]
+        gate = [f32("gate0")]
+
+        def gate_argument(t, dst):
+            nc.vector.tensor_tensor(dst, pick(b_win[t], list6), b_plain[t], ALU.subtract)
+
+        def gate_sigmoid(t, src):
+            nc.scalar.activation(gate[t][:], src, ACT.Sigmoid, scale=-1.0)
+
+        def a_window(t):
+            nc.scalar.activation(a_win[t][:, PLANE], a_banks[t][:], ACT.Copy, scale=-1.0 if t < TURNED else 1.0)
+
+        gate_argument(0, a_win[0][:, SPARE])
+        gate_sigmoid(0, a_win[0][:, SPARE])
+        gate_argument(1, a_win[1][:, SPARE])
+        z_codes = tile("z_codes", S, U32)
+        z_scales = tile("z_scales", S, U8)
+        nc.vector.quantize_mx(z_codes[:].bitcast(X4), z_scales[:], z_bf[:])
+        for t in range(PACK):
+            product(a_banks[t][:], w2_codes, w2_scales, t, z_codes[:], z_scales[:])
+        gate.extend([f32("gate1", S, "w2_scales"), f32("gate2", S, "z_codes")])
+        a_win.append(f32("a_win2", 2 * S, "z_bf"))
+        a_win.append(f32("a_win3", 2 * S, "diff3"))
+        a_window(0)
+        a_window(1)
+        gate_sigmoid(1, a_win[1][:, SPARE])
+        gate_argument(2, a_win[3][:, SPARE])
+        gate_sigmoid(2, a_win[3][:, SPARE])
+        a_window(2)
+        a_window(3)
+        gate_argument(3, a_win[2][:, SPARE])
+
+        out_planes = out.rearrange("(p t) j -> p t j", t=PACK)
+        kept = [f32(f"kept{t}") for t in range(PACK)]
+        taken = [f32(f"taken{t}") for t in range(PACK)]
+        result = [f32("result0")[:], f32("result1")[:], a_win[2][:, SPARE], f32("result3")[:]]
+
+        def keep(t):
+            nc.vector.scalar_tensor_tensor(kept[t][:], gate[t][:], 1.0, a_banks[t][:], ALU.subtract, ALU.mult)
+
+        def finish_on_vector(t, cols):
+            nc.vector.tensor_tensor(result[t][:, cols], taken[t][:, cols], kept[t][:, cols], ALU.subtract)
+            nc.sync.dma_start(out_planes[:, t, cols], result[t][:, cols])
+
+        def finish_by_transposes(t):
+            turned = f32(f"turned{t}")
+            for h in range(2):
+                total = bank(f"total{t}_{h}", HALF, f"bankB{h}")
+                for c in range(HALF // P):
+                    cols = slice(h * HALF + c * P, h * HALF + (c + 1) * P)
+                    dst = total[:, c * P:(c + 1) * P]
+                    nc.tensor.matmul(dst, lhsT=kept[t][:, cols], rhs=ident[:], start=True, stop=False, is_transpose=True)
+                    nc.tensor.matmul(dst, lhsT=taken[t][:, cols], rhs=ident[:], start=False, stop=True, is_transpose=True)
+                nc.scalar.activation(turned[:, half(h)], total[:], ACT.Copy, scale=-1.0)
+            back = bank(f"back{t}", S, f"bankA{t}")
+            for c in range(S // P):
+                cols = slice(c * P, (c + 1) * P)
+                nc.tensor.transpose(back[:, cols], turned[:, cols], ident[:])
+            nc.scalar.activation(result[t], back[:], ACT.Copy)
+            nc.scalar.dma_start(out_planes[:, t, :], result[t])
+
+        for t in range(LAST):
+            keep(t)
+            nc.vector.tensor_tensor(taken[t][:], pick(a_win[t], list5), gate[t][:], ALU.mult)
+            if t < TURNED:
+                finish_by_transposes(t)
+            if t == 0:
+                gate.append(f32("gate3", S, "kept0"))
+                gate_sigmoid(LAST, a_win[2][:, SPARE])
+        keep(LAST)
+        nc.vector.tensor_tensor(taken[LAST][:, half(0)], pick_half(a_win[LAST], list5, 0), gate[LAST][:, half(0)], ALU.mult)
+        finish_on_vector(LAST - 1, PLANE)
+        nc.vector.tensor_tensor(taken[LAST][:, half(1)], pick_half(a_win[LAST], list5, 1), gate[LAST][:, half(1)], ALU.mult)
+        for h in range(2):
+            finish_on_vector(LAST, half(h))

from contextlib import ExitStack

import concourse.mybir as mybir
from concourse.masks import make_identity

T, S, H = 2048, 512, 512
FLOPS = 3 * 2 * 512 * 512 * 512

F32 = mybir.dt.float32
BF16 = mybir.dt.bfloat16
I32 = mybir.dt.int32
U32 = mybir.dt.uint32
U16 = mybir.dt.uint16
U8 = mybir.dt.uint8
X4 = mybir.dt.float8_e4m3fn_x4
ALU = mybir.AluOpType
ACT = mybir.ActivationFunctionType

P = 128
PACK = 4
LAST = PACK - 1
HALF = S // 2
HALF_COLS = HALF // 16
PLANE = slice(0, S)
SPARE = slice(S, 2 * S)
W1_ON_VECTOR = 64
TURNED = 2


def tile_picked_tiepullblapunder_none_p_kernel(tc, x_words, x_scales, w1, gn, w2, offs, n1, n2, n3, n4, n5, n6, out):
    nc = tc.nc
    with ExitStack() as ctx:
        lists = ctx.enter_context(tc.tile_pool(name="lists", bufs=1))
        sb = ctx.enter_context(tc.tile_pool(name="sb", bufs=1))
        ps = ctx.enter_context(tc.psum_pool(name="ps", bufs=1))

        def load_list(name, src):
            offsets = lists.tile([P, S // 16], U16, name=name)
            nc.sync.dma_start(offsets[:], src)
            return offsets

        def half(h):
            return slice(h * HALF, (h + 1) * HALF)

        def half_words(h):
            return slice(h * HALF * PACK, (h + 1) * HALF * PACK)

        def plane(t):
            return slice(t * S, (t + 1) * S)

        def pick(window, offsets):
            return window[:].indirect(offsets[:])

        def pick_half(window, offsets, h):
            return window[:].indirect(offsets[:, h * HALF_COLS:(h + 1) * HALF_COLS])

        def tile(name, width, dtype, tag=None):
            return sb.tile([P, width], dtype, name=name, tag=tag or name, align_bytes=64)

        def f32(name, width=S, tag=None):
            return tile(name, width, F32, tag)

        def bank(name, width, tag):
            return ps.tile([P, width], F32, name=name, tag=tag)

        def product(dst, w_codes, w_scales, t, codes, scales):
            cols = slice(t * P, (t + 1) * P)
            nc.tensor.matmul_mx(dst, lhsT=w_codes[:, cols].bitcast(X4), lhsT_scale=w_scales[:, cols],
                                rhs=codes.bitcast(X4), rhs_scale=scales, start=True, stop=True)

        def scaled(dst, src, factor, t):
            nc.scalar.activation(dst, src, ACT.Copy, scale=factor[:, t:t + 1])

        def words_view(words):
            return words.rearrange("p (c i t) -> p c t i", i=4, t=PACK)

        def planes_view(planes):
            return planes.rearrange("p (t c i) -> p c t i", i=4, t=PACK)

        x_scale_table = tile("x_scale_table", T, U8)
        nc.gpsimd.memset(x_scale_table[:].bitcast(I32), 0)
        gain = f32("gain", PACK)
        x_scale_rows = tile("x_scale_rows", T // 4, I32)
        nc.scalar.dma_start(gain[:], gn.rearrange("(p t) o -> p (t o)", t=PACK))
        idx = load_list("idx", offs)
        for q in range(4):
            queue = nc.scalar if q < 2 else nc.sync
            queue.dma_start(x_scale_rows[32 * q:32 * q + 4, :], x_scales[0, 4 * q:4 * q + 4, :].bitcast(I32))
        w1_raw = sb.tile([P, PACK, H], F32, name="w1_raw", tag="w_raw", align_bytes=64)
        nc.sync.dma_start(w1_raw[:], w1.rearrange("(p j) c -> p j c", j=PACK))
        x_word_table = tile("x_word_table", T, U32)
        nc.sync.dma_start(x_word_table[:].bitcast(I32), x_words[0].rearrange("p n r -> p (n r)").bitcast(I32))
        list3 = load_list("list3", n3)
        list4 = load_list("list4", n4)
        list1 = load_list("list1", n1)
        list2 = load_list("list2", n2)
        list6 = load_list("list6", n6)
        list5 = load_list("list5", n5)

        gain_step2, gain_sign, gain_abs, gain_abs75 = (f32(n, PACK) for n in ("gain_step2", "gain_sign", "gain_abs", "gain_abs75"))
        nc.scalar.activation(gain_abs[:], gain[:], ACT.Abs)
        nc.scalar.activation(gain_abs75[:], gain[:], ACT.Abs, scale=0.75)
        nc.gpsimd.tensor_scalar(gain_step2[:], gain[:], 0.0, 2.0, ALU.is_ge, ALU.mult)
        nc.gpsimd.tensor_scalar(gain_sign[:], gain_step2[:], -1.0, None, ALU.add)
        ident = f32("ident", P)
        make_identity(nc, ident[:])

        for q in range(4):
            nc.vector.tensor_copy(x_scale_table[32 * q:32 * q + 4, :].bitcast(I32), x_scale_rows[32 * q:32 * q + 4, :])
        x_picked_scales = tile("x_picked_scales", S, U8)
        nc.vector.tensor_copy(x_picked_scales[:], pick(x_scale_table, idx))
        w1_bf = tile("w1_bf", PACK * H, BF16)
        w1_to = w1_bf[:].rearrange("p (t m j) -> p m j t", t=PACK, j=PACK)
        w1_from = w1_raw[:].rearrange("p j (m t) -> p m j t", t=PACK)
        nc.vector.tensor_copy(w1_to[:, 0:W1_ON_VECTOR], w1_from[:, 0:W1_ON_VECTOR])
        nc.scalar.copy(w1_to[:, W1_ON_VECTOR:P], w1_from[:, W1_ON_VECTOR:P])
        w2_raw = sb.tile([P, PACK, H], F32, name="w2_raw", tag="w_raw", align_bytes=64)
        nc.sync.dma_start(w2_raw[:], w2.rearrange("(p j) c -> p j c", j=PACK))
        w1_codes = tile("w1_codes", H, U32)
        w1_scales = tile("w1_scales", H, U8)
        nc.vector.quantize_mx(w1_codes[:].bitcast(X4), w1_scales[:], w1_bf[:])
        x_picked_words = tile("x_picked_words", S, U32, "w1_bf")
        for h in range(2):
            nc.vector.tensor_copy(x_picked_words[:, half(h)], pick_half(x_word_table, idx, h))

        y0_banks = [bank("y0_0", HALF, "bankA0"), bank("y0_1", HALF, "bankB0")]
        for h in range(2):
            product(y0_banks[h][:], w1_codes, w1_scales, 0, x_picked_words[:, half(h)], x_picked_scales[:, half(h)])
        y_banks = {}
        for t in range(1, PACK):
            y_banks[t] = bank(f"y{t}", S, f"bankA{t}")
            product(y_banks[t][:], w1_codes, w1_scales, t, x_picked_words[:], x_picked_scales[:])

        h_win = [f32("h_win0")] + [f32(f"h_win{t}", 2 * S) for t in range(1, PACK)]
        h75_win = [f32(f"h75_win{t}", 2 * S) for t in range(PACK)]
        b_win = [f32(f"b_win{t}", 2 * S) for t in range(PACK)]
        h_plain = [h_win[1][:, SPARE], h_win[2][:, SPARE], h75_win[1][:, SPARE], h75_win[0][:, SPARE]]
        for window in (h_win[3], h75_win[2], h75_win[3]):
            nc.vector.memset(window[:, SPARE], 0.0)

        scaled(h_win[0][:, half(0)], y0_banks[0][:], gain_abs, 0)
        scaled(h_win[0][:, half(1)], y0_banks[1][:], gain_abs, 0)
        nc.vector.tensor_scalar(h_plain[0][:, half(0)], y0_banks[0][:], gain_abs[:, 0:1], None, ALU.mult)
        scaled(h_plain[0][:, half(1)], y0_banks[1][:], gain_abs, 0)
        scaled(h_win[1][:, PLANE], y_banks[1][:], gain_abs, 1)
        scaled(h_plain[1], y_banks[1][:], gain_abs, 1)
        for t in range(2, PACK):
            scaled(h_win[t][:, PLANE], y_banks[t][:], gain_abs, t)
            nc.sync.dma_start(h_plain[t], h_win[t][:, PLANE])
        for h in range(2):
            scaled(h75_win[0][:, half(h)], y0_banks[h][:], gain_abs75, 0)
        for t in range(1, LAST):
            scaled(h75_win[t][:, PLANE], y_banks[t][:], gain_abs75, t)

        w2_signed = tile("w2_signed", PACK * H, BF16)
        for j in range(PACK):
            scaled(w2_signed[:, j * H:(j + 1) * H], w2_raw[:, j, :], gain_sign, j)
        scaled(h75_win[LAST][:, PLANE], y_banks[LAST][:], gain_abs75, LAST)
        w2_bf = tile("w2_bf", PACK * H, BF16)
        nc.scalar.copy(w2_bf[:].rearrange("p (t m j) -> p m j t", t=PACK, j=PACK),
                       w2_signed[:].rearrange("p (j m t) -> p m j t", j=PACK, t=PACK))

        diff3 = f32("diff3", PACK * S)
        diff4 = f32("diff4", PACK * S)
        for h in range(2):
            nc.vector.tensor_tensor(diff3[:, half(h)], pick_half(h_win[0], list3, h), h_plain[0][:, half(h)], ALU.subtract)
            nc.vector.tensor_tensor(diff4[:, half(h)], pick_half(h_win[0], list4, h), h_plain[0][:, half(h)], ALU.subtract)
        for t in range(1, PACK):
            nc.vector.tensor_tensor(diff3[:, plane(t)], pick(h_win[t], list3), h_plain[t], ALU.subtract)
            nc.vector.tensor_tensor(diff4[:, plane(t)], pick(h_win[t], list4), h_plain[t], ALU.subtract)
        diff3_bf = tile("diff3_bf", PACK * S, BF16, "w_raw")
        nc.scalar.copy(words_view(diff3_bf[:]), planes_view(diff3[:]))
        diff4_bf = [tile("diff4_bf0", PACK * HALF, BF16, "w2_signed"),
                    tile("diff4_bf1", PACK * HALF, BF16, "diff3")]
        for h in range(2):
            nc.scalar.copy(words_view(diff4_bf[h][:]), planes_view(diff4[:])[:, h * HALF // 4:(h + 1) * HALF // 4])
        min_bf = tile("min_bf", PACK * S, BF16)

        part_rest = f32("part_rest", LAST * S, f"h_win{LAST}")
        part = [b_win[0][:, SPARE]] + [part_rest[:, plane(t)] for t in range(LAST)]
        for t in range(PACK):
            nc.vector.tensor_tensor(part[t], pick(h75_win[t], list1), h_plain[t], ALU.subtract)

        min_codes = tile("min_codes", S, U32)
        min_scales = tile("min_scales", S, U8)
        for h in range(2):
            nc.vector.tensor_tensor(min_bf[:, half_words(h)], diff3_bf[:, half_words(h)], diff4_bf[h][:], ALU.min)
        w2_codes = tile("w2_codes", H, U32, "diff4")
        w2_scales = tile("w2_scales", H, U8)
        nc.vector.quantize_mx(w2_codes[:].bitcast(X4), w2_scales[:], w2_bf[:])
        nc.vector.quantize_mx(min_codes[:].bitcast(X4), min_scales[:], min_bf[:])
        b_banks = [bank(f"b{t}", S, f"bankB{t}") for t in range(PACK)]
        for t in range(PACK):
            product(b_banks[t][:], w2_codes, w2_scales, t, min_codes[:], min_scales[:])
        b_plain = [b_win[t + 1][:, SPARE] for t in range(LAST)] + [f32("b_plain_last")[:]]
        for t in range(PACK):
            nc.scalar.activation(b_win[t][:, PLANE], b_banks[t][:], ACT.Copy)
            nc.sync.dma_start(b_plain[t], b_win[t][:, PLANE])

        z_f32 = f32("z_f32", PACK * S, "diff3")
        z_bf = tile("z_bf", PACK * S, BF16)
        for h in range(2):
            for t in range(PACK):
                at = (h * PACK + t) * HALF
                nc.vector.tensor_tensor(z_f32[:, at:at + HALF], pick_half(h75_win[t], list2, h), part[t][:, half(h)], ALU.add)
            nc.scalar.copy(words_view(z_bf[:, half_words(h)]), planes_view(z_f32[:, half_words(h)]))

        a_banks = [bank(f"a{t}", S, f"bankA{t}") for t in range(PACK)]
        a_win = [f32("a_win0", 2 * S), f32("a_win1", 2 * S)]
        gate = [f32("gate0")]

        def gate_argument(t, dst):
            nc.vector.tensor_tensor(dst, pick(b_win[t], list6), b_plain[t], ALU.subtract)

        def gate_sigmoid(t, src):
            nc.scalar.activation(gate[t][:], src, ACT.Sigmoid, scale=-1.0)

        def a_window(t):
            nc.scalar.activation(a_win[t][:, PLANE], a_banks[t][:], ACT.Copy, scale=-1.0 if t < TURNED else 1.0)

        gate_argument(0, a_win[0][:, SPARE])
        gate_sigmoid(0, a_win[0][:, SPARE])
        gate_argument(1, a_win[1][:, SPARE])
        z_codes = tile("z_codes", S, U32)
        z_scales = tile("z_scales", S, U8)
        nc.vector.quantize_mx(z_codes[:].bitcast(X4), z_scales[:], z_bf[:])
        for t in range(PACK):
            product(a_banks[t][:], w2_codes, w2_scales, t, z_codes[:], z_scales[:])
        gate.extend([f32("gate1", S, "w2_scales"), f32("gate2", S, "z_codes")])
        a_win.append(f32("a_win2", 2 * S, "z_bf"))
        a_win.append(f32("a_win3", 2 * S, "diff3"))
        a_window(0)
        a_window(1)
        gate_sigmoid(1, a_win[1][:, SPARE])
        gate_argument(2, a_win[3][:, SPARE])
        gate_sigmoid(2, a_win[3][:, SPARE])
        a_window(2)
        a_window(3)
        gate_argument(3, a_win[2][:, SPARE])

        out_planes = out.rearrange("(p t) j -> p t j", t=PACK)
        kept = [f32(f"kept{t}") for t in range(PACK)]
        taken = [f32(f"taken{t}") for t in range(PACK)]
        result = [f32("result0")[:], f32("result1")[:], a_win[2][:, SPARE], f32("result3")[:]]

        def keep(t):
            nc.vector.scalar_tensor_tensor(kept[t][:], gate[t][:], 1.0, a_banks[t][:], ALU.subtract, ALU.mult)

        def finish_on_vector(t, cols):
            nc.vector.tensor_tensor(result[t][:, cols], taken[t][:, cols], kept[t][:, cols], ALU.subtract)
            nc.sync.dma_start(out_planes[:, t, cols], result[t][:, cols])

        def finish_by_transposes(t):
            turned = f32(f"turned{t}")
            for h in range(2):
                total = bank(f"total{t}_{h}", HALF, f"bankB{h}")
                for c in range(HALF // P):
                    cols = slice(h * HALF + c * P, h * HALF + (c + 1) * P)
                    dst = total[:, c * P:(c + 1) * P]
                    nc.tensor.matmul(dst, lhsT=kept[t][:, cols], rhs=ident[:], start=True, stop=False, is_transpose=True)
                    nc.tensor.matmul(dst, lhsT=taken[t][:, cols], rhs=ident[:], start=False, stop=True, is_transpose=True)
                nc.scalar.activation(turned[:, half(h)], total[:], ACT.Copy, scale=-1.0)
            back = bank(f"back{t}", S, f"bankA{t}")
            for c in range(S // P):
                cols = slice(c * P, (c + 1) * P)
                nc.tensor.transpose(back[:, cols], turned[:, cols], ident[:])
            nc.scalar.activation(result[t], back[:], ACT.Copy)
            nc.scalar.dma_start(out_planes[:, t, :], result[t])

        for t in range(LAST):
            keep(t)
            nc.vector.tensor_tensor(taken[t][:], pick(a_win[t], list5), gate[t][:], ALU.mult)
            if t < TURNED:
                finish_by_transposes(t)
            if t == 0:
                gate.append(f32("gate3", S, "kept0"))
                gate_sigmoid(LAST, a_win[2][:, SPARE])
        keep(LAST)
        nc.vector.tensor_tensor(taken[LAST][:, half(0)], pick_half(a_win[LAST], list5, 0), gate[LAST][:, half(0)], ALU.mult)
        finish_on_vector(LAST - 1, PLANE)
        nc.vector.tensor_tensor(taken[LAST][:, half(1)], pick_half(a_win[LAST], list5, 1), gate[LAST][:, half(1)], ALU.mult)
        for h in range(2):
            finish_on_vector(LAST, half(h))
